import numpy as np
import ml_dtypes


def mxq(x, axis, fmt="e4m3"):
    dtype, down = {"e4m3": (ml_dtypes.float8_e4m3fn, 7), "e5m2": (ml_dtypes.float8_e5m2, 14)}[fmt]
    v = np.moveaxis(np.asarray(x, np.float32).astype(ml_dtypes.bfloat16).astype(np.float64), axis, -1)
    blocks = v.reshape(v.shape[:-1] + (-1, 32))
    amax = np.abs(blocks).max(-1, keepdims=True)
    byte = np.maximum(np.where(amax > 0, np.frexp(amax)[1] - 1 + 127, 0) - down, 1)
    scale = np.exp2(byte - 127.0)
    codes = (blocks / scale).astype(np.float32).astype(dtype).astype(np.float64)
    return np.moveaxis((codes * scale).reshape(v.shape), -1, axis)


WIDE = False


def mx_kscale(k):
    if not WIDE:
        return np.ones(k)
    levels = np.array([10, -10, 5, -5, 0])
    if k % 512:
        return np.exp2(np.random.permutation(np.resize(levels, k // 32))).repeat(32)
    a = np.empty((k // 512, 16))
    for p in range(k // 512):
        a[p, :8] = np.random.permutation(np.resize(levels, 8))
        for g in range(8):
            far = levels[np.abs(levels - a[p, g]) >= 10]
            a[p, g + 8] = far[np.random.randint(len(far))]
    return np.exp2(a.ravel()).repeat(32)


def f64(x):
    return np.asarray(x).astype(np.float64)


def striped(idx):
    return np.tile(idx.reshape(-1, 16).T, (8, 1)).astype(np.uint16)


def unstriped(offs):
    return offs[:16].T.reshape(-1).astype(np.int64)


E2M1 = np.array([0.0, 0.5, 1.0, 1.5, 2.0, 3.0, 4.0, 6.0, -0.0, -0.5, -1.0, -1.5, -2.0, -3.0, -4.0, -6.0])


def pack_weight(w, fmt):
    k, n = w.shape
    w = f64(np.asarray(w, np.float32).astype(ml_dtypes.bfloat16)).reshape(k // 32, 32, n)
    amax = np.abs(w).max(1)
    if fmt == "e4m3":
        byte = np.frexp(amax)[1] - 1 + 127 - 7
    else:
        mant, ex = np.frexp(amax / 6.0)
        byte = np.where(mant > 0.5, ex, ex - 1) + 127
    byte = np.clip(np.where(amax > 0, byte, 1), 1, 254)
    scaled = (w * np.exp2(127.0 - byte)[:, None, :]).reshape(k, n).astype(np.float32)
    by_word = np.ascontiguousarray(scaled.reshape(k // 512, 128, 4, n).transpose(0, 1, 3, 2))
    if fmt == "e4m3":
        words = by_word.astype(ml_dtypes.float8_e4m3fn).view(np.uint8)
    else:
        c = by_word.astype(ml_dtypes.float4_e2m1fn).view(np.uint8) & 0xF
        words = (c[..., 0::2] | (c[..., 1::2] << 4)).reshape(k // 512, 128, 2 * n)
    return np.ascontiguousarray(words), np.ascontiguousarray(byte.astype(np.uint8).reshape(k // 512, 16, n))


def unpack_weight(words, scales, fmt):
    g, _, n = scales.shape
    words = np.ascontiguousarray(words).reshape(g, 128, n, -1)
    if fmt == "e4m3":
        vals = words.view(ml_dtypes.float8_e4m3fn).astype(np.float64)
    else:
        nib = np.empty((g, 128, n, 4), np.uint8)
        nib[..., 0::2] = words & 0xF
        nib[..., 1::2] = words >> 4
        vals = E2M1[nib]
    vals = vals * np.repeat(np.exp2(scales.astype(np.float64) - 127.0), 8, axis=1)[..., None]
    return vals.transpose(0, 1, 3, 2).reshape(g * 512, n)


K, T, E, C, H, N = 1024, 512, 4, 256, 512, 512


def by_expert(wq, xq):
    return np.concatenate([wq[e].T @ xq[:, e * C:(e + 1) * C] for e in range(E)], axis=1)


def setup_inputs():
    n = np.random.standard_normal
    s = mx_kscale(K)
    u = mx_kscale(H)
    first = np.random.permutation(np.repeat(np.arange(E), T // E))
    second = (first + 1 + np.random.permutation(np.repeat(np.arange(E - 1), -(-T // (E - 1)))[:T])) % E
    while np.bincount(second, minlength=E).max() != T // E:
        load = np.bincount(second, minlength=E); hi, lo = int(load.argmax()), int(load.argmin())
        t = np.flatnonzero((second == hi) & (first != lo))[0]; second[t] = lo
    slot_token = np.empty(E * C, np.int64); pos = np.empty((2, T), np.int64); fill = np.zeros(E, np.int64)
    place = np.stack([np.random.permutation(C) for _ in range(E)])
    for r, deal in enumerate((first, second)):
        for t in np.random.permutation(T):
            e = deal[t]; j = e * C + place[e, fill[e]]; fill[e] += 1; slot_token[j] = t; pos[r, t] = j
    g = np.random.uniform(0.2, 0.8, T)
    partner = np.concatenate([np.random.permutation(T) for _ in range(-(-E * C // T))])[:E * C]
    x = pack_weight(n((K, T)) * s[:, None], "e4m3")
    wp = [pack_weight(m, "e4m3") for m in n((E, K, H)) / np.sqrt(K) / s[None, :, None] * u]
    return {
        "x_words": x[0],
        "x_scales": x[1],
        "w1": (n((E, K, H)) / np.sqrt(K) / s[None, :, None] * u).astype(np.float32),
        "wp_words": np.stack([m[0] for m in wp]),
        "wp_scales": np.stack([m[1] for m in wp]),
        "w2": (n((E, H, N)) / np.sqrt(H) / u[None, :, None]).astype(np.float32),
        "gate": np.stack([np.tile(g, (128, 1)), np.tile(1.0 - g, (128, 1))]).astype(np.float32),
        "offs": striped(slot_token),
        "pos1": striped(pos[0]),
        "pos2": striped(pos[1]),
        "offs2": striped(partner),
    }


def reference(x_words, x_scales, w1, wp_words, wp_scales, w2, gate, offs, pos1, pos2, offs2):
    w1q = mxq(f64(w1), 1, "e4m3")
    wp = np.stack([unpack_weight(wp_words[e], wp_scales[e], "e4m3") for e in range(E)])
    w2q = mxq(f64(w2), 1, "e4m3")
    idx, idx2 = unstriped(offs), unstriped(offs2)
    x = unpack_weight(x_words, x_scales, "e4m3")
    h = by_expert(w1q, x[:, idx]) + by_expert(wp, x[:, idx2])
    y = by_expert(w2q, mxq(h, 0, "e4m3"))
    out = sum(f64(gate[r, :1]) * y[:, unstriped(p)] for r, p in enumerate((pos1, pos2)))
    return out

@@ -1,0 +1,191 @@
+from contextlib import ExitStack
+
+import concourse.mybir as mybir
+from concourse.masks import make_identity
+
+K, T, E, C, H, N = 1024, 512, 4, 256, 512, 512
+FLOPS = 2 * E * C * (2 * K * H + H * N)
+
+F32 = mybir.dt.float32
+BF16 = mybir.dt.bfloat16
+I32 = mybir.dt.int32
+U32 = mybir.dt.uint32
+U16 = mybir.dt.uint16
+U8 = mybir.dt.uint8
+FP8X4 = mybir.dt.float8_e4m3fn_x4
+MULT = mybir.AluOpType.mult
+ADD = mybir.AluOpType.add
+
+P = 128
+PACK = 4
+K_PASS = P * PACK
+PASSES = K // K_PASS
+SLOTS = E * C
+LIST_COLS = C // 16
+ROW_TILES = N // P
+SCALAR_COLS = (384, 384, 384, 384, 384, 384, 320, 256)
+
+
+def interleave(engine_copy, grouped, raw, lo, hi):
+    engine_copy(
+        out=grouped[:, lo:hi, :].rearrange("p (c i) j -> p c j i", i=4),
+        in_=raw[:, :, lo:hi].rearrange("p j (c i) -> p c j i", i=4),
+    )
+
+
+def tile_moe_duo_none_kernel(
+    tc, x_words, x_scales, w1, wp_words, wp_scales, w2, gate, offs, pos1, pos2, offs2, out
+):
+    nc = tc.nc
+    with ExitStack() as ctx:
+        keep = ctx.enter_context(tc.tile_pool(name="keep", bufs=1))
+        raw_pool = ctx.enter_context(tc.tile_pool(name="raw", bufs=6))
+        ring = ctx.enter_context(tc.tile_pool(name="ring", bufs=3))
+        h_psum = ctx.enter_context(tc.psum_pool(name="h_psum", bufs=2))
+        y_psum = ctx.enter_context(tc.psum_pool(name="y_psum", bufs=4))
+
+        token_list = keep.tile([P, SLOTS // 16], U16, name="token_list")
+        partner_list = keep.tile([P, SLOTS // 16], U16, name="partner_list")
+        slot_lists = [keep.tile([P, T // 16], U16, name="slot_list%d" % r) for r in range(2)]
+        x_w = [keep.tile([P, T], I32, name="x_w%d" % s, align_bytes=64) for s in range(PASSES)]
+        x_s = keep.tile([P, T], U8, name="x_s", align_bytes=64)
+        wp_s = keep.tile([P, E * PASSES, H], U8, name="wp_s", align_bytes=64)
+        gates = keep.tile([P, 2, T], F32, name="gates")
+        ident = keep.tile([P, P], F32, name="ident")
+
+        nc.sync.dma_start(token_list[:], offs)
+        nc.sync.dma_start(x_w[0][:], x_words[0].rearrange("p t d -> p (t d)").bitcast(I32))
+        nc.sync.dma_start(partner_list[:], offs2)
+        nc.sync.dma_start(x_w[1][:], x_words[1].rearrange("p t d -> p (t d)").bitcast(I32))
+
+        nc.vector.memset(x_s[:].bitcast(I32), 0)
+        make_identity(nc, ident[:])
+        wp_scale_rows = wp_scales.rearrange("e s b i -> b (e s) i")
+
+        h_codes, h_scales = [], []
+        for e in range(E):
+            list_cols = slice(e * LIST_COLS, (e + 1) * LIST_COLS)
+            got_w = keep.tile([P, 2, PASSES, C], U32, name="got_w%d" % e, align_bytes=64)
+            got_s = keep.tile([P, 2, C], U8, name="got_s%d" % e, align_bytes=64)
+            for s in range(PASSES):
+                for side, lst in enumerate((token_list, partner_list)):
+                    nc.vector.tensor_copy(got_w[:, side, s, :], x_w[s][:].bitcast(U32).indirect(lst[:, list_cols]))
+
+            w1_codes, w1_scales = [], []
+            for s in range(PASSES):
+                raw = raw_pool.tile([P, PACK, H], F32, name="w1_raw")
+                nc.sync.dma_start(raw[:], w1[e, s * K_PASS : (s + 1) * K_PASS, :].rearrange("(p j) i -> p j i", j=PACK))
+                for q in range(4 if e == 0 else 0):
+                    if s == 0:
+                        nc.sync.dma_start(
+                            x_s[32 * q : 32 * q + 4 * PASSES, :].bitcast(I32),
+                            x_scales[:, 4 * q : 4 * q + 4, :].bitcast(I32),
+                        )
+                    else:
+                        nc.sync.dma_start(
+                            wp_s[32 * q : 32 * q + 4, :, :].bitcast(I32),
+                            wp_scale_rows[4 * q : 4 * q + 4, :, :].bitcast(I32),
+                        )
+                grouped = ring.tile([P, H, PACK], BF16, name="w1_grouped", align_bytes=64)
+                if s == 0:
+                    for side, lst in enumerate((token_list, partner_list)):
+                        nc.vector.tensor_copy(got_s[:, side, :], x_s[:].indirect(lst[:, list_cols]))
+                split = SCALAR_COLS[e * PASSES + s]
+                interleave(nc.scalar.copy, grouped, raw, 0, split)
+                interleave(nc.vector.tensor_copy, grouped, raw, split, H)
+                codes = ring.tile([P, H], U32, name="w1_codes", align_bytes=64, bufs=4)
+                scales = ring.tile([P, H], U8, name="w1_scales", align_bytes=64, bufs=4)
+                nc.vector.quantize_mx(
+                    out=codes[:].bitcast(FP8X4), scales=scales[:], in_=grouped[:].rearrange("p i j -> p (i j)")
+                )
+                w1_codes.append(codes)
+                w1_scales.append(scales)
+            wp_w = keep.tile([P, PASSES, H], I32, name="wp_w%d" % e, align_bytes=64)
+            nc.sync.dma_start(wp_w[:], wp_words[e].rearrange("s p i d -> p s (i d)").bitcast(I32))
+            if e == 0:
+                for r, pos in enumerate((pos1, pos2)):
+                    nc.sync.dma_start(slot_lists[r][:], pos)
+
+            steps = [
+                (0, 0, w1_codes[0][:], w1_scales[0][:]),
+                (1, 0, wp_w[:, 0, :], wp_s[:, e * PASSES, :]),
+                (1, 1, wp_w[:, 1, :], wp_s[:, e * PASSES + 1, :]),
+                (0, 1, w1_codes[1][:], w1_scales[1][:]),
+            ]
+            h_banks = [h_psum.tile([P, H], F32, name="h_bank") for st in range(C // P)]
+            for n, (side, s, w_codes, w_scales) in enumerate(steps):
+                for st in range(C // P):
+                    slots = slice(st * P, (st + 1) * P)
+                    nc.tensor.matmul_mx(
+                        out=h_banks[st][:],
+                        lhsT=got_w[:, side, s, slots].bitcast(FP8X4),
+                        lhsT_scale=got_s[4 * s :, side, slots],
+                        rhs=w_codes.bitcast(FP8X4),
+                        rhs_scale=w_scales,
+                        start=(n == 0),
+                        stop=(n == len(steps) - 1),
+                    )
+            turned = h_psum.tile([P, C // P, 2, P], F32, name="turned")
+            for st in range(C // P):
+                h_rows = ring.tile([P, 2, P, 2], BF16, name="h_rows")
+                copy = nc.vector.tensor_copy if (e == E - 1 and st == 1) else nc.scalar.copy
+                copy(out=h_rows[:], in_=h_banks[st][:].rearrange("s (q u d) -> s u q d", u=2, d=2))
+                for u in range(2):
+                    nc.tensor.transpose(turned[:, st, u, :], h_rows[:, u, :, :].rearrange("s q d -> s (q d)").bitcast(F32), ident[:])
+            h_grouped = ring.tile([P, C * PACK], BF16, name="h_grouped", align_bytes=64)
+            nc.scalar.copy(
+                out=h_grouped[:].bitcast(F32).rearrange("q (st s u) -> q st s u", st=C // P, u=2),
+                in_=turned[:].rearrange("q st u s -> q st s u"),
+            )
+            codes = keep.tile([P, C], U32, name="h_codes%d" % e, align_bytes=64)
+            scales = keep.tile([P, C], U8, name="h_scales%d" % e, align_bytes=64)
+            nc.vector.quantize_mx(out=codes[:].bitcast(FP8X4), scales=scales[:], in_=h_grouped[:])
+            h_codes.append(codes)
+            h_scales.append(scales)
+
+        pending = None
+        for nt in range(ROW_TILES):
+            rows = slice(nt * P, (nt + 1) * P)
+            grouped = ring.tile([P, E * P, PACK], BF16, name="w2_grouped", align_bytes=64)
+            for e in range(E):
+                raw = keep.tile([P, PACK, P], F32, name="w2_raw%d_%d" % (nt, e))
+                nc.sync.dma_start(raw[:], w2[e, :, rows].rearrange("(p j) n -> p j n", j=PACK))
+                interleave(nc.scalar.copy, grouped[:, e * P : (e + 1) * P, :], raw, 0, P)
+            if nt == 0:
+                nc.sync.dma_start(gates[:], gate.rearrange("r p t -> p r t"))
+            codes = ring.tile([P, E * P], U32, name="w2_codes", align_bytes=64)
+            scales = ring.tile([P, E * P], U8, name="w2_scales", align_bytes=64)
+            nc.vector.quantize_mx(
+                out=codes[:].bitcast(FP8X4), scales=scales[:], in_=grouped[:].rearrange("p n j -> p (n j)")
+            )
+            y = ring.tile([P, SLOTS], F32, name="y")
+            for half in range(2):
+                bank = y_psum.tile([P, 2, C], F32, name="y_bank")
+                for ee in range(2):
+                    e = 2 * half + ee
+                    cols = slice(e * P, (e + 1) * P)
+                    nc.tensor.matmul_mx(
+                        out=bank[:, ee, :],
+                        lhsT=codes[:, cols].bitcast(FP8X4),
+                        lhsT_scale=scales[:, cols],
+                        rhs=h_codes[e][:].bitcast(FP8X4),
+                        rhs_scale=h_scales[e][:],
+                        start=True,
+                        stop=True,
+                    )
+                nc.scalar.copy(out=y[:, half * 2 * C : (half + 1) * 2 * C], in_=bank[:].rearrange("p a c -> p (a c)"))
+            terms = []
+            for r in range(2):
+                term = ring.tile([P, T], F32, name="term%d" % r)
+                nc.vector.tensor_tensor(term[:], y[:].indirect(slot_lists[r][:]), gates[:, r, :], MULT)
+                terms.append(term)
+                if r == 0 and pending is not None:
+                    pending()
+
+            def finish(terms=terms, rows=rows):
+                total = ring.tile([P, T], F32, name="total")
+                nc.vector.tensor_tensor(total[:], terms[0][:], terms[1][:], ADD)
+                nc.sync.dma_start(out[rows, :], total[:])
+
+            pending = finish
+        pending()

@@ -23,13 +23,15 @@ PASSES = K // K_PASS
 SLOTS = E * C
 LIST_COLS = C // 16
 ROW_TILES = N // P
-SCALAR_COLS = (384, 384, 384, 384, 384, 384, 320, 256)
+SLOT_TILES = C // P
+SCALAR_COLS = (384, 384, 384, 384, 384, 320, 256, 160)
+STEPS = ((0, 0), (1, 0), (1, 1), (0, 1))
 
 
-def interleave(engine_copy, grouped, raw, lo, hi):
+def interleave(engine_copy, grouped, raw):
     engine_copy(
-        out=grouped[:, lo:hi, :].rearrange("p (c i) j -> p c j i", i=4),
-        in_=raw[:, :, lo:hi].rearrange("p j (c i) -> p c j i", i=4),
+        out=grouped.rearrange("p (c i) j -> p c j i", i=4),
+        in_=raw.rearrange("p j (c i) -> p c j i", i=4),
     )
 
 
@@ -39,153 +41,212 @@ def tile_moe_duo_none_kernel(
     nc = tc.nc
     with ExitStack() as ctx:
         keep = ctx.enter_context(tc.tile_pool(name="keep", bufs=1))
-        raw_pool = ctx.enter_context(tc.tile_pool(name="raw", bufs=6))
-        ring = ctx.enter_context(tc.tile_pool(name="ring", bufs=3))
-        h_psum = ctx.enter_context(tc.psum_pool(name="h_psum", bufs=2))
-        y_psum = ctx.enter_context(tc.psum_pool(name="y_psum", bufs=4))
+        ring = ctx.enter_context(tc.tile_pool(name="ring", bufs=4))
+        psum = ctx.enter_context(tc.psum_pool(name="psum", bufs=6))
 
-        token_list = keep.tile([P, SLOTS // 16], U16, name="token_list")
-        partner_list = keep.tile([P, SLOTS // 16], U16, name="partner_list")
+        def place(shape, dtype, name, tag=None):
+            return keep.tile(shape, dtype, name=name, tag=tag or name, align_bytes=64)
+
+        pair_lists = [keep.tile([P, SLOTS // 16], U16, name="pair_list%d" % side) for side in range(2)]
         slot_lists = [keep.tile([P, T // 16], U16, name="slot_list%d" % r) for r in range(2)]
-        x_w = [keep.tile([P, T], I32, name="x_w%d" % s, align_bytes=64) for s in range(PASSES)]
-        x_s = keep.tile([P, T], U8, name="x_s", align_bytes=64)
-        wp_s = keep.tile([P, E * PASSES, H], U8, name="wp_s", align_bytes=64)
-        gates = keep.tile([P, 2, T], F32, name="gates")
-        ident = keep.tile([P, P], F32, name="ident")
+        x_w = [place([P, T], I32, "x_w%d" % s) for s in range(PASSES)]
+        x_s = place([P, T], U8, "x_s")
+        wp_s = [place([P, H], U8, "wp_s%d" % pair) for pair in range(E // 2)]
+        gates = [place([P, T], F32, "gate%d" % r) for r in range(2)]
+        ident = place([P, P], F32, "ident")
 
-        nc.sync.dma_start(token_list[:], offs)
-        nc.sync.dma_start(x_w[0][:], x_words[0].rearrange("p t d -> p (t d)").bitcast(I32))
-        nc.sync.dma_start(partner_list[:], offs2)
-        nc.sync.dma_start(x_w[1][:], x_words[1].rearrange("p t d -> p (t d)").bitcast(I32))
-
+        for s, index in enumerate((offs, offs2)):
+            nc.sync.dma_start(pair_lists[s][:], index)
+            nc.sync.dma_start(x_w[s][:], x_words[s].rearrange("p t d -> p (t d)").bitcast(I32))
         nc.vector.memset(x_s[:].bitcast(I32), 0)
         make_identity(nc, ident[:])
-        wp_scale_rows = wp_scales.rearrange("e s b i -> b (e s) i")
+        gate_cols = place([P, 2, 8], F32, "gate_cols")
+        nc.sync.dma_start(gate_cols[:, :, :PACK], gate[:, 0, :].rearrange("r (p j) -> p r j", j=PACK))
+        for r in range(2):
+            spread = psum.tile([P, PACK, P], F32, name="turned", bufs=2)
+            for j in range(PACK):
+                nc.tensor.transpose(spread[:, j, :], gate_cols[:, r, j : j + 1].to_broadcast([P, P]), ident[:])
+            nc.scalar.copy(out=gates[r][:].rearrange("m (p j) -> m p j", j=PACK), in_=spread[:].rearrange("m j p -> m p j"))
+        wp_scale_rows = wp_scales.rearrange("(pair e) s b i -> pair (e s) b i", e=2)
 
-        h_codes, h_scales = [], []
+        got_w, got_s = {}, {}
+
+        def gather_words(e, steps, tag=None):
+            words = place([P, len(steps), C], U32, "got_w%d_%d" % (e, len(steps)), tag)
+            for n, (side, s) in enumerate(steps):
+                offsets = pair_lists[side][:, e * LIST_COLS : (e + 1) * LIST_COLS]
+                nc.vector.tensor_copy(words[:, n, :], x_w[s][:].bitcast(U32).indirect(offsets))
+                got_w[e, side, s] = words[:, n, :]
+
+        def gather_scales(e, tag=None):
+            scales = place([P, 2, C], U8, "got_s%d" % e, tag)
+            for side in range(2):
+                offsets = pair_lists[side][:, e * LIST_COLS : (e + 1) * LIST_COLS]
+                nc.vector.tensor_copy(scales[:, side, :], x_s[:].indirect(offsets))
+            got_s[e] = scales
+
+        def quantize(grouped, name, pool):
+            width = grouped.shape[1] // PACK
+            codes = pool.tile([P, width], U32, name=name + "_codes", align_bytes=64)
+            scales = pool.tile([P, width], U8, name=name + "_scales", align_bytes=64)
+            nc.vector.quantize_mx(out=codes[:].bitcast(FP8X4), scales=scales[:], in_=grouped)
+            return codes, scales
+
+        def load_w1(e, s):
+            split = SCALAR_COLS[e * PASSES + s]
+            rows = w1[e, s * K_PASS : (s + 1) * K_PASS, :].rearrange("(p j) i -> p j i", j=PACK)
+            raw = place([P, PACK, H], F32, "w1_raw%d_%d" % (e, s))
+            nc.sync.dma_start(raw[:], rows)
+            grouped = place([P, H, PACK], BF16, "w1_grouped%d_%d" % (e, s))
+            interleave(nc.scalar.copy, grouped[:, :split, :], raw[:, :, :split])
+            interleave(nc.vector.tensor_copy, grouped[:, split:, :], raw[:, :, split:])
+            return grouped
+
+        h_banks, turned, h_quant = {}, {}, {}
+
+        def first_layer(e):
+            h_banks[e] = [psum.tile([P, H], F32, name="bank") for st in range(SLOT_TILES)]
+            for n, (side, s) in enumerate(STEPS):
+                if side == 0:
+                    w_codes, w_scales = w1_quant[e, s][0][:], w1_quant[e, s][1][:]
+                else:
+                    w_codes, w_scales = wp_w[e, s][:], wp_s[e // 2][4 * (e % 2 * PASSES + s) :, :]
+                for st in range(SLOT_TILES):
+                    slots = slice(st * P, (st + 1) * P)
+                    nc.tensor.matmul_mx(
+                        out=h_banks[e][st][:],
+                        lhsT=got_w[e, side, s][:, slots].bitcast(FP8X4),
+                        lhsT_scale=got_s[e][4 * s :, side, slots],
+                        rhs=w_codes.bitcast(FP8X4),
+                        rhs_scale=w_scales,
+                        start=(n == 0),
+                        stop=(n == len(STEPS) - 1),
+                    )
+
+        def turn_h(e, tag, copies, banks):
+            h_rows = place([P, SLOT_TILES, 2, P, 2], BF16, "h_rows%d" % e, tag)
+            share = SLOT_TILES // banks
+            turned[e] = [psum.tile([P, share, 2, P], F32, name="turned", bufs=2) for n in range(banks)]
+            for st in range(SLOT_TILES):
+                copies[st](out=h_rows[:, st], in_=h_banks[e][st][:].rearrange("s (q u d) -> s u q d", u=2, d=2))
+                for u in range(2):
+                    words = h_rows[:, st, u].rearrange("s q d -> s (q d)").bitcast(F32)
+                    nc.tensor.transpose(turned[e][st // share][:, st % share, u, :], words, ident[:])
+
+        def quantize_h(e, tag, copies):
+            h_grouped = place([P, C * PACK], BF16, "h_grouped%d" % e, tag)
+            pairs = h_grouped[:].bitcast(F32).rearrange("q (st s u) -> q st s u", st=SLOT_TILES, u=2)
+            share = SLOT_TILES // len(copies)
+            for n, copy in enumerate(copies):
+                part = slice(n * share, (n + 1) * share)
+                copy(out=pairs[:, part], in_=turned[e][n][:].rearrange("q st u s -> q st s u"))
+            h_quant[e] = quantize(h_grouped[:], "h%d" % e, keep)
+
+        wp_w = {}
+
+        def load_wp(e, s):
+            wp_w[e, s] = place([P, H], I32, "wp_w%d_%d" % (e, s))
+            nc.sync.dma_start(wp_w[e, s][:], wp_words[e, s].rearrange("p i d -> p (i d)").bitcast(I32))
+
+        gather_words(0, STEPS)
+        gather_words(1, STEPS[:3])
+        w1_quant = {}
         for e in range(E):
-            list_cols = slice(e * LIST_COLS, (e + 1) * LIST_COLS)
-            got_w = keep.tile([P, 2, PASSES, C], U32, name="got_w%d" % e, align_bytes=64)
-            got_s = keep.tile([P, 2, C], U8, name="got_s%d" % e, align_bytes=64)
             for s in range(PASSES):
-                for side, lst in enumerate((token_list, partner_list)):
-                    nc.vector.tensor_copy(got_w[:, side, s, :], x_w[s][:].bitcast(U32).indirect(lst[:, list_cols]))
-
-            w1_codes, w1_scales = [], []
-            for s in range(PASSES):
-                raw = raw_pool.tile([P, PACK, H], F32, name="w1_raw")
-                nc.sync.dma_start(raw[:], w1[e, s * K_PASS : (s + 1) * K_PASS, :].rearrange("(p j) i -> p j i", j=PACK))
-                for q in range(4 if e == 0 else 0):
-                    if s == 0:
+                grouped = load_w1(e, s)
+                for q in range(4):
+                    if (e, s) == (0, 0):
                         nc.sync.dma_start(
                             x_s[32 * q : 32 * q + 4 * PASSES, :].bitcast(I32),
                             x_scales[:, 4 * q : 4 * q + 4, :].bitcast(I32),
                         )
-                    else:
+                    if e < E // 2 and s == 1:
                         nc.sync.dma_start(
-                            wp_s[32 * q : 32 * q + 4, :, :].bitcast(I32),
-                            wp_scale_rows[4 * q : 4 * q + 4, :, :].bitcast(I32),
+                            wp_s[e][32 * q : 32 * q + 16, :].bitcast(I32),
+                            wp_scale_rows[e, :, 4 * q : 4 * q + 4, :].bitcast(I32),
                         )
-                grouped = ring.tile([P, H, PACK], BF16, name="w1_grouped", align_bytes=64)
-                if s == 0:
-                    for side, lst in enumerate((token_list, partner_list)):
-                        nc.vector.tensor_copy(got_s[:, side, :], x_s[:].indirect(lst[:, list_cols]))
-                split = SCALAR_COLS[e * PASSES + s]
-                interleave(nc.scalar.copy, grouped, raw, 0, split)
-                interleave(nc.vector.tensor_copy, grouped, raw, split, H)
-                codes = ring.tile([P, H], U32, name="w1_codes", align_bytes=64, bufs=4)
-                scales = ring.tile([P, H], U8, name="w1_scales", align_bytes=64, bufs=4)
-                nc.vector.quantize_mx(
-                    out=codes[:].bitcast(FP8X4), scales=scales[:], in_=grouped[:].rearrange("p i j -> p (i j)")
+                if e == 0 and s == 0:
+                    gather_scales(0)
+                w1_quant[e, s] = quantize(grouped[:].rearrange("p i j -> p (i j)"), "w", ring)
+                if e + 1 < E and s == 0:
+                    gather_words(e + 1, STEPS[3:], "w1_raw%d_0" % e)
+                    gather_scales(e + 1, "w1_grouped%d_0" % e)
+                if e + 2 < E and s == 1:
+                    gather_words(e + 2, STEPS[:3], "w1_raw%d_1" % e)
+                if e > 0 and s == 0:
+                    load_wp(e - 1, 1)
+                    first_layer(e - 1)
+                    turn_h(e - 1, None, (nc.scalar.copy, nc.scalar.copy), 1)
+                if e > 0 and s == 1:
+                    quantize_h(e - 1, "w1_raw%d_1" % e if e + 1 == E else None, (nc.scalar.copy,))
+                if s == 1:
+                    load_wp(e, 0)
+            if e >= 2:
+                nc.sync.dma_start(slot_lists[e - 2][:], (pos1, pos2)[e - 2])
+        load_wp(E - 1, 1)
+        first_layer(E - 1)
+        turn_h(E - 1, None, (nc.scalar.copy, nc.vector.tensor_copy), 1)
+        quantize_h(E - 1, None, (nc.scalar.copy,))
+
+        w2_quant, ys, terms = {}, {}, {}
+
+        def cast_w2(nt, half, copy):
+            grouped = ring.tile([P, 2 * P, PACK], BF16, name="w2_grouped", align_bytes=64)
+            for n in range(2):
+                e = 2 * half + n
+                raw = place([P, PACK, P], F32, "w2_raw%d_%d" % (nt, e))
+                nc.sync.dma_start(raw[:], w2[e, :, nt * P : (nt + 1) * P].rearrange("(p j) n -> p j n", j=PACK))
+                interleave(copy, grouped[:, n * P : (n + 1) * P, :], raw[:])
+            codes, scales = quantize(grouped[:].rearrange("p n j -> p (n j)"), "w2", ring)
+            for n in range(2):
+                w2_quant[nt, 2 * half + n] = codes[:, n * P : (n + 1) * P], scales[:, n * P : (n + 1) * P]
+
+        def second_layer(nt, half, tag=None):
+            if nt not in ys:
+                ys[nt] = place([P, SLOTS], F32, "y%d" % nt, tag)
+            bank = psum.tile([P, 2, C], F32, name="bank")
+            for place_in_bank in range(2):
+                e = 2 * half + place_in_bank
+                codes, scales = w2_quant[nt, e]
+                nc.tensor.matmul_mx(
+                    out=bank[:, place_in_bank, :],
+                    lhsT=codes.bitcast(FP8X4),
+                    lhsT_scale=scales,
+                    rhs=h_quant[e][0][:].bitcast(FP8X4),
+                    rhs_scale=h_quant[e][1][:],
+                    start=True,
+                    stop=True,
                 )
-                w1_codes.append(codes)
-                w1_scales.append(scales)
-            wp_w = keep.tile([P, PASSES, H], I32, name="wp_w%d" % e, align_bytes=64)
-            nc.sync.dma_start(wp_w[:], wp_words[e].rearrange("s p i d -> p s (i d)").bitcast(I32))
-            if e == 0:
-                for r, pos in enumerate((pos1, pos2)):
-                    nc.sync.dma_start(slot_lists[r][:], pos)
+            nc.scalar.copy(out=ys[nt][:, half * 2 * C : (half + 1) * 2 * C], in_=bank[:].rearrange("p a c -> p (a c)"))
 
-            steps = [
-                (0, 0, w1_codes[0][:], w1_scales[0][:]),
-                (1, 0, wp_w[:, 0, :], wp_s[:, e * PASSES, :]),
-                (1, 1, wp_w[:, 1, :], wp_s[:, e * PASSES + 1, :]),
-                (0, 1, w1_codes[1][:], w1_scales[1][:]),
-            ]
-            h_banks = [h_psum.tile([P, H], F32, name="h_bank") for st in range(C // P)]
-            for n, (side, s, w_codes, w_scales) in enumerate(steps):
-                for st in range(C // P):
-                    slots = slice(st * P, (st + 1) * P)
-                    nc.tensor.matmul_mx(
-                        out=h_banks[st][:],
-                        lhsT=got_w[:, side, s, slots].bitcast(FP8X4),
-                        lhsT_scale=got_s[4 * s :, side, slots],
-                        rhs=w_codes.bitcast(FP8X4),
-                        rhs_scale=w_scales,
-                        start=(n == 0),
-                        stop=(n == len(steps) - 1),
-                    )
-            turned = h_psum.tile([P, C // P, 2, P], F32, name="turned")
-            for st in range(C // P):
-                h_rows = ring.tile([P, 2, P, 2], BF16, name="h_rows")
-                copy = nc.vector.tensor_copy if (e == E - 1 and st == 1) else nc.scalar.copy
-                copy(out=h_rows[:], in_=h_banks[st][:].rearrange("s (q u d) -> s u q d", u=2, d=2))
-                for u in range(2):
-                    nc.tensor.transpose(turned[:, st, u, :], h_rows[:, u, :, :].rearrange("s q d -> s (q d)").bitcast(F32), ident[:])
-            h_grouped = ring.tile([P, C * PACK], BF16, name="h_grouped", align_bytes=64)
-            nc.scalar.copy(
-                out=h_grouped[:].bitcast(F32).rearrange("q (st s u) -> q st s u", st=C // P, u=2),
-                in_=turned[:].rearrange("q st u s -> q st s u"),
-            )
-            codes = keep.tile([P, C], U32, name="h_codes%d" % e, align_bytes=64)
-            scales = keep.tile([P, C], U8, name="h_scales%d" % e, align_bytes=64)
-            nc.vector.quantize_mx(out=codes[:].bitcast(FP8X4), scales=scales[:], in_=h_grouped[:])
-            h_codes.append(codes)
-            h_scales.append(scales)
+        def fetch(nt, r, term):
+            nc.vector.tensor_tensor(term, ys[nt][:].indirect(slot_lists[r][:]), gates[r][:], MULT)
+            terms[nt, r] = term
 
-        pending = None
+        def finish(nt, total):
+            nc.vector.tensor_tensor(total, terms[nt, 0], terms[nt, 1], ADD)
+            nc.sync.dma_start(out[nt * P : (nt + 1) * P, :], total)
+
+        def row(name, tag=None):
+            return place([P, T], F32, name, tag)[:]
+
+        for half in range(2):
+            cast_w2(0, half, nc.vector.tensor_copy)
+            second_layer(0, half)
+        cast_w2(1, 0, nc.vector.tensor_copy)
+        second_layer(1, 0)
+        fetch(0, 0, row("first_term"))
         for nt in range(ROW_TILES):
-            rows = slice(nt * P, (nt + 1) * P)
-            grouped = ring.tile([P, E * P, PACK], BF16, name="w2_grouped", align_bytes=64)
-            for e in range(E):
-                raw = keep.tile([P, PACK, P], F32, name="w2_raw%d_%d" % (nt, e))
-                nc.sync.dma_start(raw[:], w2[e, :, rows].rearrange("(p j) n -> p j n", j=PACK))
-                interleave(nc.scalar.copy, grouped[:, e * P : (e + 1) * P, :], raw, 0, P)
-            if nt == 0:
-                nc.sync.dma_start(gates[:], gate.rearrange("r p t -> p r t"))
-            codes = ring.tile([P, E * P], U32, name="w2_codes", align_bytes=64)
-            scales = ring.tile([P, E * P], U8, name="w2_scales", align_bytes=64)
-            nc.vector.quantize_mx(
-                out=codes[:].bitcast(FP8X4), scales=scales[:], in_=grouped[:].rearrange("p n j -> p (n j)")
-            )
-            y = ring.tile([P, SLOTS], F32, name="y")
-            for half in range(2):
-                bank = y_psum.tile([P, 2, C], F32, name="y_bank")
-                for ee in range(2):
-                    e = 2 * half + ee
-                    cols = slice(e * P, (e + 1) * P)
-                    nc.tensor.matmul_mx(
-                        out=bank[:, ee, :],
-                        lhsT=codes[:, cols].bitcast(FP8X4),
-                        lhsT_scale=scales[:, cols],
-                        rhs=h_codes[e][:].bitcast(FP8X4),
-                        rhs_scale=h_scales[e][:],
-                        start=True,
-                        stop=True,
-                    )
-                nc.scalar.copy(out=y[:, half * 2 * C : (half + 1) * 2 * C], in_=bank[:].rearrange("p a c -> p (a c)"))
-            terms = []
-            for r in range(2):
-                term = ring.tile([P, T], F32, name="term%d" % r)
-                nc.vector.tensor_tensor(term[:], y[:].indirect(slot_lists[r][:]), gates[:, r, :], MULT)
-                terms.append(term)
-                if r == 0 and pending is not None:
-                    pending()
-
-            def finish(terms=terms, rows=rows):
-                total = ring.tile([P, T], F32, name="total")
-                nc.vector.tensor_tensor(total[:], terms[0][:], terms[1][:], ADD)
-                nc.sync.dma_start(out[rows, :], total[:])
-
-            pending = finish
-        pending()
+            if nt + 1 < ROW_TILES:
+                cast_w2(nt + 1, 1, nc.scalar.copy)
+            fetch(nt, 1, row("term%d" % nt, "w2_raw%d_3" % (nt + 1) if nt + 1 < ROW_TILES else None))
+            if nt + 2 < ROW_TILES:
+                cast_w2(nt + 2, 0, nc.scalar.copy)
+            if nt + 1 < ROW_TILES:
+                second_layer(nt + 1, 1)
+            pair = place([P, 2, T], F32, "pair%d" % nt, "w2_raw%d_1" % (nt + 2) if nt + 2 < ROW_TILES else None)
+            finish(nt, pair[:, 0, :])
+            if nt + 1 < ROW_TILES:
+                fetch(nt + 1, 0, pair[:, 1, :])
+            if nt + 2 < ROW_TILES:
+                second_layer(nt + 2, 0)

@@ -25,6 +25,7 @@ LIST_COLS = C // 16
 ROW_TILES = N // P
 SLOT_TILES = C // P
 SCALAR_COLS = (384, 384, 384, 384, 384, 320, 256, 160)
+VECTOR_W2 = ((0, 0), (0, 1), (0, 2), (0, 3), (1, 0), (1, 1), (2, 1))
 STEPS = ((0, 0), (1, 0), (1, 1), (0, 1))
 
 
@@ -161,7 +162,7 @@ def tile_moe_duo_none_kernel(
                             x_scales[:, 4 * q : 4 * q + 4, :].bitcast(I32),
                         )
                     if e < E // 2 and s == 1:
-                        nc.sync.dma_start(
+                        nc.gpsimd.dma_start(
                             wp_s[e][32 * q : 32 * q + 16, :].bitcast(I32),
                             wp_scale_rows[e, :, 4 * q : 4 * q + 4, :].bitcast(I32),
                         )
@@ -181,8 +182,6 @@ def tile_moe_duo_none_kernel(
                     quantize_h(e - 1, "w1_raw%d_1" % e if e + 1 == E else None, (nc.scalar.copy,))
                 if s == 1:
                     load_wp(e, 0)
-            if e >= 2:
-                nc.sync.dma_start(slot_lists[e - 2][:], (pos1, pos2)[e - 2])
         load_wp(E - 1, 1)
         first_layer(E - 1)
         turn_h(E - 1, None, (nc.scalar.copy, nc.vector.tensor_copy), 1)
@@ -190,26 +189,25 @@ def tile_moe_duo_none_kernel(
 
         w2_quant, ys, terms = {}, {}, {}
 
-        def cast_w2(nt, half, copy):
-            grouped = ring.tile([P, 2 * P, PACK], BF16, name="w2_grouped", align_bytes=64)
-            for n in range(2):
-                e = 2 * half + n
+        def cast_w2(nt, experts):
+            grouped = ring.tile([P, len(experts) * P, PACK], BF16, name="w2_grouped", align_bytes=64)
+            for n, e in enumerate(experts):
                 raw = place([P, PACK, P], F32, "w2_raw%d_%d" % (nt, e))
                 nc.sync.dma_start(raw[:], w2[e, :, nt * P : (nt + 1) * P].rearrange("(p j) n -> p j n", j=PACK))
+                copy = nc.vector.tensor_copy if (nt, e) in VECTOR_W2 else nc.scalar.copy
                 interleave(copy, grouped[:, n * P : (n + 1) * P, :], raw[:])
             codes, scales = quantize(grouped[:].rearrange("p n j -> p (n j)"), "w2", ring)
-            for n in range(2):
-                w2_quant[nt, 2 * half + n] = codes[:, n * P : (n + 1) * P], scales[:, n * P : (n + 1) * P]
+            for n, e in enumerate(experts):
+                w2_quant[nt, e] = codes[:, n * P : (n + 1) * P], scales[:, n * P : (n + 1) * P]
 
-        def second_layer(nt, half, tag=None):
+        def second_layer(nt, experts):
             if nt not in ys:
-                ys[nt] = place([P, SLOTS], F32, "y%d" % nt, tag)
-            bank = psum.tile([P, 2, C], F32, name="bank")
-            for place_in_bank in range(2):
-                e = 2 * half + place_in_bank
+                ys[nt] = place([P, SLOTS], F32, "y%d" % nt)
+            bank = psum.tile([P, len(experts), C], F32, name="bank")
+            for n, e in enumerate(experts):
                 codes, scales = w2_quant[nt, e]
                 nc.tensor.matmul_mx(
-                    out=bank[:, place_in_bank, :],
+                    out=bank[:, n, :],
                     lhsT=codes.bitcast(FP8X4),
                     lhsT_scale=scales,
                     rhs=h_quant[e][0][:].bitcast(FP8X4),
@@ -217,36 +215,44 @@ def tile_moe_duo_none_kernel(
                     start=True,
                     stop=True,
                 )
-            nc.scalar.copy(out=ys[nt][:, half * 2 * C : (half + 1) * 2 * C], in_=bank[:].rearrange("p a c -> p (a c)"))
+            nc.scalar.copy(
+                out=ys[nt][:, experts[0] * C : (experts[-1] + 1) * C], in_=bank[:].rearrange("p a c -> p (a c)")
+            )
 
-        def fetch(nt, r, term):
-            nc.vector.tensor_tensor(term, ys[nt][:].indirect(slot_lists[r][:]), gates[r][:], MULT)
+        def fetch(nt, r, term, lo=0, hi=T):
+            offsets = slot_lists[r][:, lo // 16 : hi // 16]
+            nc.vector.tensor_tensor(term[:, lo:hi], ys[nt][:].indirect(offsets), gates[r][:, lo:hi], MULT)
             terms[nt, r] = term
 
-        def finish(nt, total):
-            nc.vector.tensor_tensor(total, terms[nt, 0], terms[nt, 1], ADD)
-            nc.sync.dma_start(out[nt * P : (nt + 1) * P, :], total)
+        def finish(nt, total, lo=0, hi=T):
+            nc.vector.tensor_tensor(total[:, lo:hi], terms[nt, 0][:, lo:hi], terms[nt, 1][:, lo:hi], ADD)
+            nc.sync.dma_start(out[nt * P : (nt + 1) * P, lo:hi], total[:, lo:hi])
 
         def row(name, tag=None):
             return place([P, T], F32, name, tag)[:]
 
-        for half in range(2):
-            cast_w2(0, half, nc.vector.tensor_copy)
-            second_layer(0, half)
-        cast_w2(1, 0, nc.vector.tensor_copy)
-        second_layer(1, 0)
+        front, back = (0, 1), (2, 3)
+        for experts in (front, (2,), (3,)):
+            cast_w2(0, experts)
+            second_layer(0, experts)
+        for r, pos in enumerate((pos1, pos2)):
+            nc.sync.dma_start(slot_lists[r][:], pos)
+        cast_w2(1, front)
+        second_layer(1, front)
         fetch(0, 0, row("first_term"))
-        for nt in range(ROW_TILES):
-            if nt + 1 < ROW_TILES:
-                cast_w2(nt + 1, 1, nc.scalar.copy)
-            fetch(nt, 1, row("term%d" % nt, "w2_raw%d_3" % (nt + 1) if nt + 1 < ROW_TILES else None))
+        for nt in range(ROW_TILES - 1):
+            cast_w2(nt + 1, back)
+            fetch(nt, 1, row("term%d" % nt, "w2_raw%d_3" % (nt + 1)))
             if nt + 2 < ROW_TILES:
-                cast_w2(nt + 2, 0, nc.scalar.copy)
-            if nt + 1 < ROW_TILES:
-                second_layer(nt + 1, 1)
+                cast_w2(nt + 2, front)
+            second_layer(nt + 1, back)
             pair = place([P, 2, T], F32, "pair%d" % nt, "w2_raw%d_1" % (nt + 2) if nt + 2 < ROW_TILES else None)
             finish(nt, pair[:, 0, :])
-            if nt + 1 < ROW_TILES:
-                fetch(nt + 1, 0, pair[:, 1, :])
+            fetch(nt + 1, 0, pair[:, 1, :])
             if nt + 2 < ROW_TILES:
-                second_layer(nt + 2, 0)
+                second_layer(nt + 2, front)
+        last, term, total = ROW_TILES - 1, row("last_term"), row("last_total")
+        for lo, hi in ((0, 256), (256, 512)):
+            fetch(last, 1, term, lo, hi)
+        for lo, hi in ((0, 256), (256, 512)):
+            finish(last, total, lo, hi)

@@ -21,16 +21,21 @@ PACK = 4
 K_PASS = P * PACK
 PASSES = K // K_PASS
 SLOTS = E * C
-LIST_COLS = C // 16
+PER_COLUMN = 16
+QUADRANTS = 4
+SCALE_ROWS = 4
 ROW_TILES = N // P
 SLOT_TILES = C // P
-SCALAR_COLS = (384, 384, 384, 384, 384, 320, 256, 160)
-VECTOR_W2 = ((0, 0), (0, 1), (0, 2), (0, 3), (1, 0), (1, 1), (2, 1))
-STEPS = ((0, 0), (1, 0), (1, 1), (0, 1))
+TOKEN, PARTNER = 0, 1
+
+SCALAR_COLUMNS = (416, 416, 416, 416, 416, 384, 256, 160)
+VECTOR_W2_PIECES = ((0, 0), (0, 1), (0, 2), (0, 3), (1, 0), (1, 1))
+STEPS = ((TOKEN, 0), (PARTNER, 0), (PARTNER, 1), (TOKEN, 1))
+EARLY_STEPS, LATE_STEPS = STEPS[:3], STEPS[3:]
 
 
-def interleave(engine_copy, grouped, raw):
-    engine_copy(
+def interleave(copy, grouped, raw):
+    copy(
         out=grouped.rearrange("p (c i) j -> p c j i", i=4),
         in_=raw.rearrange("p j (c i) -> p c j i", i=4),
     )
@@ -43,47 +48,58 @@ def tile_moe_duo_none_kernel(
     with ExitStack() as ctx:
         keep = ctx.enter_context(tc.tile_pool(name="keep", bufs=1))
         ring = ctx.enter_context(tc.tile_pool(name="ring", bufs=4))
-        psum = ctx.enter_context(tc.psum_pool(name="psum", bufs=6))
+        psum = ctx.enter_context(tc.psum_pool(name="psum", bufs=2))
 
-        def place(shape, dtype, name, tag=None):
-            return keep.tile(shape, dtype, name=name, tag=tag or name, align_bytes=64)
+        def place(shape, dtype, name, after=None):
+            return keep.tile(shape, dtype, name=name, tag=after or name, align_bytes=64)
 
-        pair_lists = [keep.tile([P, SLOTS // 16], U16, name="pair_list%d" % side) for side in range(2)]
-        slot_lists = [keep.tile([P, T // 16], U16, name="slot_list%d" % r) for r in range(2)]
+        pair_lists = [keep.tile([P, SLOTS // PER_COLUMN], U16, name="pair_list%d" % side) for side in range(2)]
+        slot_lists = [keep.tile([P, T // PER_COLUMN], U16, name="slot_list%d" % r) for r in range(2)]
         x_w = [place([P, T], I32, "x_w%d" % s) for s in range(PASSES)]
         x_s = place([P, T], U8, "x_s")
         wp_s = [place([P, H], U8, "wp_s%d" % pair) for pair in range(E // 2)]
         gates = [place([P, T], F32, "gate%d" % r) for r in range(2)]
         ident = place([P, P], F32, "ident")
 
-        for s, index in enumerate((offs, offs2)):
-            nc.sync.dma_start(pair_lists[s][:], index)
-            nc.sync.dma_start(x_w[s][:], x_words[s].rearrange("p t d -> p (t d)").bitcast(I32))
+        for n, index in enumerate((offs, offs2)):
+            nc.sync.dma_start(pair_lists[n][:], index)
+            nc.sync.dma_start(x_w[n][:], x_words[n].rearrange("p t d -> p (t d)").bitcast(I32))
         nc.vector.memset(x_s[:].bitcast(I32), 0)
         make_identity(nc, ident[:])
-        gate_cols = place([P, 2, 8], F32, "gate_cols")
+
+        gate_cols = place([P, 2, 2 * PACK], F32, "gate_cols")
         nc.sync.dma_start(gate_cols[:, :, :PACK], gate[:, 0, :].rearrange("r (p j) -> p r j", j=PACK))
         for r in range(2):
-            spread = psum.tile([P, PACK, P], F32, name="turned", bufs=2)
+            spread = psum.tile([P, PACK, P], F32, name="turned")
             for j in range(PACK):
                 nc.tensor.transpose(spread[:, j, :], gate_cols[:, r, j : j + 1].to_broadcast([P, P]), ident[:])
-            nc.scalar.copy(out=gates[r][:].rearrange("m (p j) -> m p j", j=PACK), in_=spread[:].rearrange("m j p -> m p j"))
-        wp_scale_rows = wp_scales.rearrange("(pair e) s b i -> pair (e s) b i", e=2)
+            nc.scalar.copy(
+                out=gates[r][:].rearrange("m (p j) -> m p j", j=PACK), in_=spread[:].rearrange("m j p -> m p j")
+            )
 
-        got_w, got_s = {}, {}
+        def load_scale_rows(tile, rows):
+            height = rows.shape[0] * SCALE_ROWS
+            for q in range(QUADRANTS):
+                nc.sync.dma_start(
+                    tile[32 * q : 32 * q + height, :].bitcast(I32),
+                    rows[:, SCALE_ROWS * q : SCALE_ROWS * (q + 1), :].bitcast(I32),
+                )
 
-        def gather_words(e, steps, tag=None):
-            words = place([P, len(steps), C], U32, "got_w%d_%d" % (e, len(steps)), tag)
+        got_w, got_s, wp_w, w1_quant = {}, {}, {}, {}
+
+        def expert_offsets(e, side):
+            return pair_lists[side][:, e * C // PER_COLUMN : (e + 1) * C // PER_COLUMN]
+
+        def gather_words(e, steps, after=None):
+            words = place([P, len(steps), C], U32, "got_w%d_%d" % (e, len(steps)), after)
             for n, (side, s) in enumerate(steps):
-                offsets = pair_lists[side][:, e * LIST_COLS : (e + 1) * LIST_COLS]
-                nc.vector.tensor_copy(words[:, n, :], x_w[s][:].bitcast(U32).indirect(offsets))
+                nc.vector.tensor_copy(words[:, n, :], x_w[s][:].bitcast(U32).indirect(expert_offsets(e, side)))
                 got_w[e, side, s] = words[:, n, :]
 
-        def gather_scales(e, tag=None):
-            scales = place([P, 2, C], U8, "got_s%d" % e, tag)
-            for side in range(2):
-                offsets = pair_lists[side][:, e * LIST_COLS : (e + 1) * LIST_COLS]
-                nc.vector.tensor_copy(scales[:, side, :], x_s[:].indirect(offsets))
+        def gather_scales(e, after=None):
+            scales = place([P, 2, C], U8, "got_s%d" % e, after)
+            for side in (TOKEN, PARTNER):
+                nc.vector.tensor_copy(scales[:, side, :], x_s[:].indirect(expert_offsets(e, side)))
             got_s[e] = scales
 
         def quantize(grouped, name, pool):
@@ -94,107 +110,95 @@ def tile_moe_duo_none_kernel(
             return codes, scales
 
         def load_w1(e, s):
-            split = SCALAR_COLS[e * PASSES + s]
-            rows = w1[e, s * K_PASS : (s + 1) * K_PASS, :].rearrange("(p j) i -> p j i", j=PACK)
+            split = SCALAR_COLUMNS[e * PASSES + s]
             raw = place([P, PACK, H], F32, "w1_raw%d_%d" % (e, s))
-            nc.sync.dma_start(raw[:], rows)
+            nc.sync.dma_start(raw[:], w1[e, s * K_PASS : (s + 1) * K_PASS, :].rearrange("(p j) i -> p j i", j=PACK))
             grouped = place([P, H, PACK], BF16, "w1_grouped%d_%d" % (e, s))
             interleave(nc.scalar.copy, grouped[:, :split, :], raw[:, :, :split])
             interleave(nc.vector.tensor_copy, grouped[:, split:, :], raw[:, :, split:])
             return grouped
 
-        h_banks, turned, h_quant = {}, {}, {}
+        def load_wp(e, s):
+            wp_w[e, s] = place([P, H], I32, "wp_w%d_%d" % (e, s))
+            nc.sync.dma_start(wp_w[e, s][:], wp_words[e, s].rearrange("p i d -> p (i d)").bitcast(I32))
 
-        def first_layer(e):
-            h_banks[e] = [psum.tile([P, H], F32, name="bank") for st in range(SLOT_TILES)]
+        turned, h_quant = {}, {}
+
+        def first_layer(e, copies):
+            name, bufs = ("h_bank", 2) if e + 1 < E else ("y_bank", 4)
+            banks = [psum.tile([P, H], F32, name=name, bufs=bufs) for st in range(SLOT_TILES)]
             for n, (side, s) in enumerate(STEPS):
-                if side == 0:
+                if side == TOKEN:
                     w_codes, w_scales = w1_quant[e, s][0][:], w1_quant[e, s][1][:]
                 else:
-                    w_codes, w_scales = wp_w[e, s][:], wp_s[e // 2][4 * (e % 2 * PASSES + s) :, :]
+                    w_codes, w_scales = wp_w[e, s][:], wp_s[e // 2][SCALE_ROWS * (e % 2 * PASSES + s) :, :]
                 for st in range(SLOT_TILES):
                     slots = slice(st * P, (st + 1) * P)
                     nc.tensor.matmul_mx(
-                        out=h_banks[e][st][:],
+                        out=banks[st][:],
                         lhsT=got_w[e, side, s][:, slots].bitcast(FP8X4),
-                        lhsT_scale=got_s[e][4 * s :, side, slots],
+                        lhsT_scale=got_s[e][SCALE_ROWS * s :, side, slots],
                         rhs=w_codes.bitcast(FP8X4),
                         rhs_scale=w_scales,
                         start=(n == 0),
                         stop=(n == len(STEPS) - 1),
                     )
-
-        def turn_h(e, tag, copies, banks):
-            h_rows = place([P, SLOT_TILES, 2, P, 2], BF16, "h_rows%d" % e, tag)
-            share = SLOT_TILES // banks
-            turned[e] = [psum.tile([P, share, 2, P], F32, name="turned", bufs=2) for n in range(banks)]
+            h_rows = place([P, SLOT_TILES, 2, P, 2], BF16, "h_rows%d" % e)
+            turned[e] = psum.tile([P, SLOT_TILES, 2, P], F32, name="turned")
             for st in range(SLOT_TILES):
-                copies[st](out=h_rows[:, st], in_=h_banks[e][st][:].rearrange("s (q u d) -> s u q d", u=2, d=2))
+                copies[st](out=h_rows[:, st], in_=banks[st][:].rearrange("s (q u d) -> s u q d", u=2, d=2))
                 for u in range(2):
-                    words = h_rows[:, st, u].rearrange("s q d -> s (q d)").bitcast(F32)
-                    nc.tensor.transpose(turned[e][st // share][:, st % share, u, :], words, ident[:])
+                    pairs = h_rows[:, st, u].rearrange("s q d -> s (q d)").bitcast(F32)
+                    nc.tensor.transpose(turned[e][:, st, u, :], pairs, ident[:])
 
-        def quantize_h(e, tag, copies):
-            h_grouped = place([P, C * PACK], BF16, "h_grouped%d" % e, tag)
-            pairs = h_grouped[:].bitcast(F32).rearrange("q (st s u) -> q st s u", st=SLOT_TILES, u=2)
-            share = SLOT_TILES // len(copies)
-            for n, copy in enumerate(copies):
-                part = slice(n * share, (n + 1) * share)
-                copy(out=pairs[:, part], in_=turned[e][n][:].rearrange("q st u s -> q st s u"))
+        def quantize_h(e, after=None):
+            h_grouped = place([P, C * PACK], BF16, "h_grouped%d" % e, after)
+            nc.scalar.copy(
+                out=h_grouped[:].bitcast(F32).rearrange("q (st s u) -> q st s u", st=SLOT_TILES, u=2),
+                in_=turned[e][:].rearrange("q st u s -> q st s u"),
+            )
             h_quant[e] = quantize(h_grouped[:], "h%d" % e, keep)
 
-        wp_w = {}
-
-        def load_wp(e, s):
-            wp_w[e, s] = place([P, H], I32, "wp_w%d_%d" % (e, s))
-            nc.sync.dma_start(wp_w[e, s][:], wp_words[e, s].rearrange("p i d -> p (i d)").bitcast(I32))
-
+        wp_scale_rows = wp_scales.rearrange("(pair e) s b i -> pair (e s) b i", e=2)
         gather_words(0, STEPS)
-        gather_words(1, STEPS[:3])
-        w1_quant = {}
+        gather_words(1, EARLY_STEPS)
         for e in range(E):
-            for s in range(PASSES):
-                grouped = load_w1(e, s)
-                for q in range(4):
-                    if (e, s) == (0, 0):
-                        nc.sync.dma_start(
-                            x_s[32 * q : 32 * q + 4 * PASSES, :].bitcast(I32),
-                            x_scales[:, 4 * q : 4 * q + 4, :].bitcast(I32),
-                        )
-                    if e < E // 2 and s == 1:
-                        nc.gpsimd.dma_start(
-                            wp_s[e][32 * q : 32 * q + 16, :].bitcast(I32),
-                            wp_scale_rows[e, :, 4 * q : 4 * q + 4, :].bitcast(I32),
-                        )
-                if e == 0 and s == 0:
-                    gather_scales(0)
-                w1_quant[e, s] = quantize(grouped[:].rearrange("p i j -> p (i j)"), "w", ring)
-                if e + 1 < E and s == 0:
-                    gather_words(e + 1, STEPS[3:], "w1_raw%d_0" % e)
-                    gather_scales(e + 1, "w1_grouped%d_0" % e)
-                if e + 2 < E and s == 1:
-                    gather_words(e + 2, STEPS[:3], "w1_raw%d_1" % e)
-                if e > 0 and s == 0:
-                    load_wp(e - 1, 1)
-                    first_layer(e - 1)
-                    turn_h(e - 1, None, (nc.scalar.copy, nc.scalar.copy), 1)
-                if e > 0 and s == 1:
-                    quantize_h(e - 1, "w1_raw%d_1" % e if e + 1 == E else None, (nc.scalar.copy,))
-                if s == 1:
-                    load_wp(e, 0)
+            grouped = load_w1(e, 0)
+            if e == 0:
+                load_scale_rows(x_s, x_scales)
+                gather_scales(0)
+            w1_quant[e, 0] = quantize(grouped[:].rearrange("p i j -> p (i j)"), "w1", ring)
+            if e + 1 < E:
+                gather_words(e + 1, LATE_STEPS, "w1_raw%d_0" % e)
+                gather_scales(e + 1, "w1_grouped%d_0" % e)
+            if e > 0:
+                load_wp(e - 1, 1)
+                first_layer(e - 1, (nc.scalar.copy, nc.scalar.copy))
+
+            grouped = load_w1(e, 1)
+            if e < len(wp_s):
+                load_scale_rows(wp_s[e], wp_scale_rows[e])
+            w1_quant[e, 1] = quantize(grouped[:].rearrange("p i j -> p (i j)"), "w1", ring)
+            if e + 2 < E:
+                gather_words(e + 2, EARLY_STEPS, "w1_raw%d_1" % e)
+            if e > 0:
+                quantize_h(e - 1, "w1_raw%d_1" % e if e + 1 == E else None)
+            load_wp(e, 0)
+            if e >= E - 2:
+                r = e - (E - 2)
+                nc.sync.dma_start(slot_lists[r][:], (pos1, pos2)[r])
         load_wp(E - 1, 1)
-        first_layer(E - 1)
-        turn_h(E - 1, None, (nc.scalar.copy, nc.vector.tensor_copy), 1)
-        quantize_h(E - 1, None, (nc.scalar.copy,))
+        first_layer(E - 1, (nc.scalar.copy, nc.vector.tensor_copy))
+        quantize_h(E - 1)
 
         w2_quant, ys, terms = {}, {}, {}
 
-        def cast_w2(nt, experts):
+        def quantize_w2(nt, experts):
             grouped = ring.tile([P, len(experts) * P, PACK], BF16, name="w2_grouped", align_bytes=64)
             for n, e in enumerate(experts):
                 raw = place([P, PACK, P], F32, "w2_raw%d_%d" % (nt, e))
                 nc.sync.dma_start(raw[:], w2[e, :, nt * P : (nt + 1) * P].rearrange("(p j) n -> p j n", j=PACK))
-                copy = nc.vector.tensor_copy if (nt, e) in VECTOR_W2 else nc.scalar.copy
+                copy = nc.vector.tensor_copy if (nt, e) in VECTOR_W2_PIECES else nc.scalar.copy
                 interleave(copy, grouped[:, n * P : (n + 1) * P, :], raw[:])
             codes, scales = quantize(grouped[:].rearrange("p n j -> p (n j)"), "w2", ring)
             for n, e in enumerate(experts):
@@ -203,7 +207,7 @@ def tile_moe_duo_none_kernel(
         def second_layer(nt, experts):
             if nt not in ys:
                 ys[nt] = place([P, SLOTS], F32, "y%d" % nt)
-            bank = psum.tile([P, len(experts), C], F32, name="bank")
+            bank = psum.tile([P, len(experts), C], F32, name="y_bank", bufs=4)
             for n, e in enumerate(experts):
                 codes, scales = w2_quant[nt, e]
                 nc.tensor.matmul_mx(
@@ -220,7 +224,7 @@ def tile_moe_duo_none_kernel(
             )
 
         def fetch(nt, r, term, lo=0, hi=T):
-            offsets = slot_lists[r][:, lo // 16 : hi // 16]
+            offsets = slot_lists[r][:, lo // PER_COLUMN : hi // PER_COLUMN]
             nc.vector.tensor_tensor(term[:, lo:hi], ys[nt][:].indirect(offsets), gates[r][:, lo:hi], MULT)
             terms[nt, r] = term
 
@@ -228,31 +232,31 @@ def tile_moe_duo_none_kernel(
             nc.vector.tensor_tensor(total[:, lo:hi], terms[nt, 0][:, lo:hi], terms[nt, 1][:, lo:hi], ADD)
             nc.sync.dma_start(out[nt * P : (nt + 1) * P, lo:hi], total[:, lo:hi])
 
-        def row(name, tag=None):
-            return place([P, T], F32, name, tag)[:]
+        def row(name, after=None):
+            return place([P, T], F32, name, after)[:]
 
         front, back = (0, 1), (2, 3)
-        for experts in (front, (2,), (3,)):
-            cast_w2(0, experts)
+        for experts in (front, back[:1], back[1:]):
+            quantize_w2(0, experts)
             second_layer(0, experts)
-        for r, pos in enumerate((pos1, pos2)):
-            nc.sync.dma_start(slot_lists[r][:], pos)
-        cast_w2(1, front)
+        quantize_w2(1, front)
         second_layer(1, front)
         fetch(0, 0, row("first_term"))
         for nt in range(ROW_TILES - 1):
-            cast_w2(nt + 1, back)
-            fetch(nt, 1, row("term%d" % nt, "w2_raw%d_3" % (nt + 1)))
-            if nt + 2 < ROW_TILES:
-                cast_w2(nt + 2, front)
+            two_ahead = nt + 2 < ROW_TILES
+            quantize_w2(nt + 1, back)
+            fetch(nt, 1, row("term%d" % nt, "w2_raw%d_%d" % (nt + 1, back[-1])))
+            if two_ahead:
+                quantize_w2(nt + 2, front)
             second_layer(nt + 1, back)
-            pair = place([P, 2, T], F32, "pair%d" % nt, "w2_raw%d_1" % (nt + 2) if nt + 2 < ROW_TILES else None)
-            finish(nt, pair[:, 0, :])
-            fetch(nt + 1, 0, pair[:, 1, :])
-            if nt + 2 < ROW_TILES:
+            both = place([P, 2, T], F32, "both%d" % nt, "w2_raw%d_%d" % (nt + 2, front[-1]) if two_ahead else None)
+            finish(nt, both[:, 0, :])
+            fetch(nt + 1, 0, both[:, 1, :])
+            if two_ahead:
                 second_layer(nt + 2, front)
-        last, term, total = ROW_TILES - 1, row("last_term"), row("last_total")
-        for lo, hi in ((0, 256), (256, 512)):
-            fetch(last, 1, term, lo, hi)
-        for lo, hi in ((0, 256), (256, 512)):
-            finish(last, total, lo, hi)
+        term, total = row("last_term"), row("last_total")
+        halves = ((0, T // 2), (T // 2, T))
+        for lo, hi in halves:
+            fetch(ROW_TILES - 1, 1, term, lo, hi)
+        for lo, hi in halves:
+            finish(ROW_TILES - 1, total, lo, hi)

from contextlib import ExitStack

import concourse.mybir as mybir
from concourse.masks import make_identity

K, T, E, C, H, N = 1024, 512, 4, 256, 512, 512
FLOPS = 2 * E * C * (2 * K * H + H * N)

F32 = mybir.dt.float32
BF16 = mybir.dt.bfloat16
I32 = mybir.dt.int32
U32 = mybir.dt.uint32
U16 = mybir.dt.uint16
U8 = mybir.dt.uint8
FP8X4 = mybir.dt.float8_e4m3fn_x4
MULT = mybir.AluOpType.mult
ADD = mybir.AluOpType.add

P = 128
PACK = 4
K_PASS = P * PACK
PASSES = K // K_PASS
SLOTS = E * C
PER_COLUMN = 16
QUADRANTS = 4
SCALE_ROWS = 4
ROW_TILES = N // P
SLOT_TILES = C // P
TOKEN, PARTNER = 0, 1

SCALAR_COLUMNS = (416, 416, 416, 416, 416, 384, 256, 160)
VECTOR_W2_PIECES = ((0, 0), (0, 1), (0, 2), (0, 3), (1, 0), (1, 1))
STEPS = ((TOKEN, 0), (PARTNER, 0), (PARTNER, 1), (TOKEN, 1))
EARLY_STEPS, LATE_STEPS = STEPS[:3], STEPS[3:]


def interleave(copy, grouped, raw):
    copy(
        out=grouped.rearrange("p (c i) j -> p c j i", i=4),
        in_=raw.rearrange("p j (c i) -> p c j i", i=4),
    )


def tile_moe_duo_none_kernel(
    tc, x_words, x_scales, w1, wp_words, wp_scales, w2, gate, offs, pos1, pos2, offs2, out
):
    nc = tc.nc
    with ExitStack() as ctx:
        keep = ctx.enter_context(tc.tile_pool(name="keep", bufs=1))
        ring = ctx.enter_context(tc.tile_pool(name="ring", bufs=4))
        psum = ctx.enter_context(tc.psum_pool(name="psum", bufs=2))

        def place(shape, dtype, name, after=None):
            return keep.tile(shape, dtype, name=name, tag=after or name, align_bytes=64)

        pair_lists = [keep.tile([P, SLOTS // PER_COLUMN], U16, name="pair_list%d" % side) for side in range(2)]
        slot_lists = [keep.tile([P, T // PER_COLUMN], U16, name="slot_list%d" % r) for r in range(2)]
        x_w = [place([P, T], I32, "x_w%d" % s) for s in range(PASSES)]
        x_s = place([P, T], U8, "x_s")
        wp_s = [place([P, H], U8, "wp_s%d" % pair) for pair in range(E // 2)]
        gates = [place([P, T], F32, "gate%d" % r) for r in range(2)]
        ident = place([P, P], F32, "ident")

        for n, index in enumerate((offs, offs2)):
            nc.sync.dma_start(pair_lists[n][:], index)
            nc.sync.dma_start(x_w[n][:], x_words[n].rearrange("p t d -> p (t d)").bitcast(I32))
        nc.vector.memset(x_s[:].bitcast(I32), 0)
        make_identity(nc, ident[:])

        gate_cols = place([P, 2, 2 * PACK], F32, "gate_cols")
        nc.sync.dma_start(gate_cols[:, :, :PACK], gate[:, 0, :].rearrange("r (p j) -> p r j", j=PACK))
        for r in range(2):
            spread = psum.tile([P, PACK, P], F32, name="turned")
            for j in range(PACK):
                nc.tensor.transpose(spread[:, j, :], gate_cols[:, r, j : j + 1].to_broadcast([P, P]), ident[:])
            nc.scalar.copy(
                out=gates[r][:].rearrange("m (p j) -> m p j", j=PACK), in_=spread[:].rearrange("m j p -> m p j")
            )

        def load_scale_rows(tile, rows):
            height = rows.shape[0] * SCALE_ROWS
            for q in range(QUADRANTS):
                nc.sync.dma_start(
                    tile[32 * q : 32 * q + height, :].bitcast(I32),
                    rows[:, SCALE_ROWS * q : SCALE_ROWS * (q + 1), :].bitcast(I32),
                )

        got_w, got_s, wp_w, w1_quant = {}, {}, {}, {}

        def expert_offsets(e, side):
            return pair_lists[side][:, e * C // PER_COLUMN : (e + 1) * C // PER_COLUMN]

        def gather_words(e, steps, after=None):
            words = place([P, len(steps), C], U32, "got_w%d_%d" % (e, len(steps)), after)
            for n, (side, s) in enumerate(steps):
                nc.vector.tensor_copy(words[:, n, :], x_w[s][:].bitcast(U32).indirect(expert_offsets(e, side)))
                got_w[e, side, s] = words[:, n, :]

        def gather_scales(e, after=None):
            scales = place([P, 2, C], U8, "got_s%d" % e, after)
            for side in (TOKEN, PARTNER):
                nc.vector.tensor_copy(scales[:, side, :], x_s[:].indirect(expert_offsets(e, side)))
            got_s[e] = scales

        def quantize(grouped, name, pool):
            width = grouped.shape[1] // PACK
            codes = pool.tile([P, width], U32, name=name + "_codes", align_bytes=64)
            scales = pool.tile([P, width], U8, name=name + "_scales", align_bytes=64)
            nc.vector.quantize_mx(out=codes[:].bitcast(FP8X4), scales=scales[:], in_=grouped)
            return codes, scales

        def load_w1(e, s):
            split = SCALAR_COLUMNS[e * PASSES + s]
            raw = place([P, PACK, H], F32, "w1_raw%d_%d" % (e, s))
            nc.sync.dma_start(raw[:], w1[e, s * K_PASS : (s + 1) * K_PASS, :].rearrange("(p j) i -> p j i", j=PACK))
            grouped = place([P, H, PACK], BF16, "w1_grouped%d_%d" % (e, s))
            interleave(nc.scalar.copy, grouped[:, :split, :], raw[:, :, :split])
            interleave(nc.vector.tensor_copy, grouped[:, split:, :], raw[:, :, split:])
            return grouped

        def load_wp(e, s):
            wp_w[e, s] = place([P, H], I32, "wp_w%d_%d" % (e, s))
            nc.sync.dma_start(wp_w[e, s][:], wp_words[e, s].rearrange("p i d -> p (i d)").bitcast(I32))

        turned, h_quant = {}, {}

        def first_layer(e, copies):
            name, bufs = ("h_bank", 2) if e + 1 < E else ("y_bank", 4)
            banks = [psum.tile([P, H], F32, name=name, bufs=bufs) for st in range(SLOT_TILES)]
            for n, (side, s) in enumerate(STEPS):
                if side == TOKEN:
                    w_codes, w_scales = w1_quant[e, s][0][:], w1_quant[e, s][1][:]
                else:
                    w_codes, w_scales = wp_w[e, s][:], wp_s[e // 2][SCALE_ROWS * (e % 2 * PASSES + s) :, :]
                for st in range(SLOT_TILES):
                    slots = slice(st * P, (st + 1) * P)
                    nc.tensor.matmul_mx(
                        out=banks[st][:],
                        lhsT=got_w[e, side, s][:, slots].bitcast(FP8X4),
                        lhsT_scale=got_s[e][SCALE_ROWS * s :, side, slots],
                        rhs=w_codes.bitcast(FP8X4),
                        rhs_scale=w_scales,
                        start=(n == 0),
                        stop=(n == len(STEPS) - 1),
                    )
            h_rows = place([P, SLOT_TILES, 2, P, 2], BF16, "h_rows%d" % e)
            turned[e] = psum.tile([P, SLOT_TILES, 2, P], F32, name="turned")
            for st in range(SLOT_TILES):
                copies[st](out=h_rows[:, st], in_=banks[st][:].rearrange("s (q u d) -> s u q d", u=2, d=2))
                for u in range(2):
                    pairs = h_rows[:, st, u].rearrange("s q d -> s (q d)").bitcast(F32)
                    nc.tensor.transpose(turned[e][:, st, u, :], pairs, ident[:])

        def quantize_h(e, after=None):
            h_grouped = place([P, C * PACK], BF16, "h_grouped%d" % e, after)
            nc.scalar.copy(
                out=h_grouped[:].bitcast(F32).rearrange("q (st s u) -> q st s u", st=SLOT_TILES, u=2),
                in_=turned[e][:].rearrange("q st u s -> q st s u"),
            )
            h_quant[e] = quantize(h_grouped[:], "h%d" % e, keep)

        wp_scale_rows = wp_scales.rearrange("(pair e) s b i -> pair (e s) b i", e=2)
        gather_words(0, STEPS)
        gather_words(1, EARLY_STEPS)
        for e in range(E):
            grouped = load_w1(e, 0)
            if e == 0:
                load_scale_rows(x_s, x_scales)
                gather_scales(0)
            w1_quant[e, 0] = quantize(grouped[:].rearrange("p i j -> p (i j)"), "w1", ring)
            if e + 1 < E:
                gather_words(e + 1, LATE_STEPS, "w1_raw%d_0" % e)
                gather_scales(e + 1, "w1_grouped%d_0" % e)
            if e > 0:
                load_wp(e - 1, 1)
                first_layer(e - 1, (nc.scalar.copy, nc.scalar.copy))

            grouped = load_w1(e, 1)
            if e < len(wp_s):
                load_scale_rows(wp_s[e], wp_scale_rows[e])
            w1_quant[e, 1] = quantize(grouped[:].rearrange("p i j -> p (i j)"), "w1", ring)
            if e + 2 < E:
                gather_words(e + 2, EARLY_STEPS, "w1_raw%d_1" % e)
            if e > 0:
                quantize_h(e - 1, "w1_raw%d_1" % e if e + 1 == E else None)
            load_wp(e, 0)
            if e >= E - 2:
                r = e - (E - 2)
                nc.sync.dma_start(slot_lists[r][:], (pos1, pos2)[r])
        load_wp(E - 1, 1)
        first_layer(E - 1, (nc.scalar.copy, nc.vector.tensor_copy))
        quantize_h(E - 1)

        w2_quant, ys, terms = {}, {}, {}

        def quantize_w2(nt, experts):
            grouped = ring.tile([P, len(experts) * P, PACK], BF16, name="w2_grouped", align_bytes=64)
            for n, e in enumerate(experts):
                raw = place([P, PACK, P], F32, "w2_raw%d_%d" % (nt, e))
                nc.sync.dma_start(raw[:], w2[e, :, nt * P : (nt + 1) * P].rearrange("(p j) n -> p j n", j=PACK))
                copy = nc.vector.tensor_copy if (nt, e) in VECTOR_W2_PIECES else nc.scalar.copy
                interleave(copy, grouped[:, n * P : (n + 1) * P, :], raw[:])
            codes, scales = quantize(grouped[:].rearrange("p n j -> p (n j)"), "w2", ring)
            for n, e in enumerate(experts):
                w2_quant[nt, e] = codes[:, n * P : (n + 1) * P], scales[:, n * P : (n + 1) * P]

        def second_layer(nt, experts):
            if nt not in ys:
                ys[nt] = place([P, SLOTS], F32, "y%d" % nt)
            bank = psum.tile([P, len(experts), C], F32, name="y_bank", bufs=4)
            for n, e in enumerate(experts):
                codes, scales = w2_quant[nt, e]
                nc.tensor.matmul_mx(
                    out=bank[:, n, :],
                    lhsT=codes.bitcast(FP8X4),
                    lhsT_scale=scales,
                    rhs=h_quant[e][0][:].bitcast(FP8X4),
                    rhs_scale=h_quant[e][1][:],
                    start=True,
                    stop=True,
                )
            nc.scalar.copy(
                out=ys[nt][:, experts[0] * C : (experts[-1] + 1) * C], in_=bank[:].rearrange("p a c -> p (a c)")
            )

        def fetch(nt, r, term, lo=0, hi=T):
            offsets = slot_lists[r][:, lo // PER_COLUMN : hi // PER_COLUMN]
            nc.vector.tensor_tensor(term[:, lo:hi], ys[nt][:].indirect(offsets), gates[r][:, lo:hi], MULT)
            terms[nt, r] = term

        def finish(nt, total, lo=0, hi=T):
            nc.vector.tensor_tensor(total[:, lo:hi], terms[nt, 0][:, lo:hi], terms[nt, 1][:, lo:hi], ADD)
            nc.sync.dma_start(out[nt * P : (nt + 1) * P, lo:hi], total[:, lo:hi])

        def row(name, after=None):
            return place([P, T], F32, name, after)[:]

        front, back = (0, 1), (2, 3)
        for experts in (front, back[:1], back[1:]):
            quantize_w2(0, experts)
            second_layer(0, experts)
        quantize_w2(1, front)
        second_layer(1, front)
        fetch(0, 0, row("first_term"))
        for nt in range(ROW_TILES - 1):
            two_ahead = nt + 2 < ROW_TILES
            quantize_w2(nt + 1, back)
            fetch(nt, 1, row("term%d" % nt, "w2_raw%d_%d" % (nt + 1, back[-1])))
            if two_ahead:
                quantize_w2(nt + 2, front)
            second_layer(nt + 1, back)
            both = place([P, 2, T], F32, "both%d" % nt, "w2_raw%d_%d" % (nt + 2, front[-1]) if two_ahead else None)
            finish(nt, both[:, 0, :])
            fetch(nt + 1, 0, both[:, 1, :])
            if two_ahead:
                second_layer(nt + 2, front)
        term, total = row("last_term"), row("last_total")
        halves = ((0, T // 2), (T // 2, T))
        for lo, hi in halves:
            fetch(ROW_TILES - 1, 1, term, lo, hi)
        for lo, hi in halves:
            finish(ROW_TILES - 1, total, lo, hi)
